import numpy as np
import ml_dtypes


def mxq(x, axis, fmt="e4m3"):
    dtype, down = {"e4m3": (ml_dtypes.float8_e4m3fn, 7), "e5m2": (ml_dtypes.float8_e5m2, 14)}[fmt]
    v = np.moveaxis(np.asarray(x, np.float32).astype(ml_dtypes.bfloat16).astype(np.float64), axis, -1)
    blocks = v.reshape(v.shape[:-1] + (-1, 32))
    amax = np.abs(blocks).max(-1, keepdims=True)
    byte = np.maximum(np.where(amax > 0, np.frexp(amax)[1] - 1 + 127, 0) - down, 1)
    scale = np.exp2(byte - 127.0)
    codes = (blocks / scale).astype(np.float32).astype(dtype).astype(np.float64)
    return np.moveaxis((codes * scale).reshape(v.shape), -1, axis)


WIDE = False


def mx_kscale(k):
    if not WIDE:
        return np.ones(k)
    levels = np.array([10, -10, 5, -5, 0])
    if k % 512:
        return np.exp2(np.random.permutation(np.resize(levels, k // 32))).repeat(32)
    a = np.empty((k // 512, 16))
    for p in range(k // 512):
        a[p, :8] = np.random.permutation(np.resize(levels, 8))
        for g in range(8):
            far = levels[np.abs(levels - a[p, g]) >= 10]
            a[p, g + 8] = far[np.random.randint(len(far))]
    return np.exp2(a.ravel()).repeat(32)


def f64(x):
    return np.asarray(x).astype(np.float64)


def striped(idx):
    return np.tile(idx.reshape(-1, 16).T, (8, 1)).astype(np.uint16)


def unstriped(offs):
    return offs[:16].T.reshape(-1).astype(np.int64)


def pack_weight(w):
    k, n = w.shape
    w = f64(np.asarray(w, np.float32).astype(ml_dtypes.bfloat16)).reshape(k // 32, 32, n)
    amax = np.abs(w).max(1)
    byte = np.clip(np.where(amax > 0, np.frexp(amax)[1] - 1 + 127 - 7, 1), 1, 254)
    scaled = (w * np.exp2(127.0 - byte)[:, None, :]).reshape(k, n).astype(np.float32)
    words = np.ascontiguousarray(scaled.reshape(k // 512, 128, 4, n).transpose(0, 1, 3, 2)).astype(ml_dtypes.float8_e4m3fn).view(np.uint8)
    return words, np.ascontiguousarray(byte.astype(np.uint8).reshape(k // 512, 16, n))


def unpack_weight(words, scales):
    g, p, n, _ = words.shape
    vals = np.ascontiguousarray(words).view(ml_dtypes.float8_e4m3fn).astype(np.float64) * np.repeat(np.exp2(scales.astype(np.float64) - 127.0), 8, axis=1)[..., None]
    return vals.transpose(0, 1, 3, 2).reshape(g * 512, n)


K, T, S, N = 512, 4096, 1024, 512


def setup_inputs():
    n = np.random.standard_normal
    s = mx_kscale(K)[:, None]
    c = mx_kscale(S)
    packed_xT = pack_weight(n((K, T)) * s)
    return {
        "x_words": packed_xT[0],
        "x_scales": packed_xT[1],
        "w1": (n((K, N)) / np.sqrt(K) / s).astype(np.float32),
        "wgt": (np.random.uniform(0.5, 1.0, (S, 1)) * c[:, None] / np.sqrt(S)).astype(np.float32),
        "inv": (np.random.uniform(0.6, 1.4, (S, 1)) / c[:, None]).astype(np.float32),
        "old": (n((N, N)) * 0.2 + np.eye(N)).astype(np.float32),
        "offs": striped(np.random.permutation(T)[:S]),
    }


def reference(x_words, x_scales, w1, wgt, inv, old, offs):
    xq = unpack_weight(x_words, x_scales)[:, unstriped(offs)]
    w1q = mxq(f64(w1), 0, "e4m3")
    y = xq.T @ w1q
    a = f64(wgt) * y
    vv = f64(inv) * y
    return 0.95 * f64(old) + 0.05 * ((mxq(a, 0, "e4m3").T @ mxq(vv, 0, "e4m3")))

@@ -1,0 +1,236 @@
+from contextlib import ExitStack
+
+import concourse.mybir as mybir
+from concourse.masks import make_identity
+
+K, T, S, N = 512, 4096, 1024, 512
+FLOPS = 2 * S * K * N + 2 * S * N * N
+
+F32 = mybir.dt.float32
+BF16 = mybir.dt.bfloat16
+I32 = mybir.dt.int32
+U32 = mybir.dt.uint32
+U16 = mybir.dt.uint16
+U8 = mybir.dt.uint8
+FP8X4 = mybir.dt.float8_e4m3fn_x4
+COPY = mybir.ActivationFunctionType.Copy
+MULT = mybir.AluOpType.mult
+ADD = mybir.AluOpType.add
+
+P = 128
+PACK = 4
+PASSES = S // (P * PACK)
+SLOTS = PASSES * PACK
+RUN = 8
+HALF = N // 2
+KEEP, GAIN = 0.95, 0.05
+A, VV = 0, 1
+LAST16 = P - 16
+
+
+def interleave_views(grouped, planes):
+    return (
+        grouped.rearrange("p (c i t) -> p c t i", i=4, t=PACK),
+        planes.rearrange("p t (c i) -> p c t i", i=4),
+    )
+
+
+def tile_picked_ykfac_lin_p_kernel(
+    tc, x_words, x_scales, w1, wgt, inv, old, offs, out
+):
+    nc = tc.nc
+    with ExitStack() as ctx:
+        sb = ctx.enter_context(tc.tile_pool(name="sb", bufs=1))
+        ps = ctx.enter_context(tc.psum_pool(name="ps", bufs=1))
+
+        def bank(b, name, cols=N):
+            return ps.tile([P, cols], F32, name=name, tag="bank%d" % b)
+
+        offsets = sb.tile([P, S // 16], U16, name="offsets")
+        nc.sync.dma_start(offsets[:], offs)
+        word_table = sb.tile([P, T], U32, name="word_table", tag="table", align_bytes=64)
+        nc.sync.dma_start(
+            word_table[:].bitcast(I32), x_words[0].rearrange("p n t -> p (n t)").bitcast(I32)
+        )
+        w_rows = w1.rearrange("(p j) n -> p j n", j=PACK)
+        w_raw = []
+        for h in range(2):
+            w_half = sb.tile([P, PACK, HALF], F32, name="w_raw%d" % h, align_bytes=64)
+            nc.sync.dma_start(w_half[:], w_rows[:, :, h * HALF : (h + 1) * HALF])
+            w_raw.append(w_half)
+
+        scale_table = sb.tile([P, T], U8, name="scale_table", align_bytes=64)
+        nc.scalar.dma_start(scale_table[LAST16:P, :].bitcast(I32), x_scales[0].bitcast(I32))
+        nc.vector.memset(scale_table[0:LAST16, :].bitcast(I32), 0)
+
+        coef_rows = sb.tile([P, P], F32, name="coef_rows", align_bytes=64)
+        for o, vec in ((A, wgt), (VV, inv)):
+            nc.scalar.dma_start(
+                coef_rows[LAST16 + o * SLOTS : LAST16 + (o + 1) * SLOTS, :].rearrange("s (q r) -> s q r", r=RUN),
+                vec.rearrange("(q s r) o -> s q (r o)", s=SLOTS, r=RUN),
+            )
+        x_scale = sb.tile([P, S], U8, name="x_scale", align_bytes=64)
+        nc.gpsimd.memset(x_scale[:].bitcast(I32), 0)
+        ident = sb.tile([P, P], F32, name="ident", align_bytes=64)
+        make_identity(nc, ident[:])
+        nc.scalar.activation(coef_rows[0:LAST16, :], ident[0:LAST16, :], COPY)
+        coef_ps = bank(7, "coef_ps", P)
+        nc.tensor.transpose(coef_ps[:], coef_rows[:], ident[:])
+        coef = sb.tile([P, 2 * SLOTS], F32, name="coef", align_bytes=64)
+        nc.scalar.activation(coef[:], coef_ps[:, LAST16:P], COPY)
+
+        picked_scales = sb.tile([P, S], U8, name="picked_scales", align_bytes=64)
+        nc.vector.tensor_copy(picked_scales[:], scale_table[:].indirect(offsets[:]))
+        dealt_scales = sb.tile([P, S], U8, name="dealt_scales", align_bytes=64)
+        nc.vector.tensor_copy(
+            dealt_scales[:].bitcast(I32).rearrange("p (s q w) -> p s q w", s=SLOTS, w=RUN // 4),
+            picked_scales[:].bitcast(I32).rearrange("p (q s w) -> p s q w", s=SLOTS, w=RUN // 4),
+        )
+        for quad in range(4):
+            nc.scalar.dma_start(
+                x_scale[32 * quad : 32 * quad + 4, :].bitcast(I32),
+                dealt_scales[LAST16 + 4 * quad : LAST16 + 4 * (quad + 1), :].bitcast(I32),
+            )
+
+        x_codes = sb.tile([P, S], U32, name="x_codes", align_bytes=64)
+        nc.vector.tensor_copy(
+            x_codes[:].rearrange("p (s q r) -> p q s r", s=SLOTS, r=RUN),
+            word_table[:].indirect(offsets[:]),
+        )
+
+        old_sb = sb.tile([P, N // P, N], F32, name="old_sb", tag="table", align_bytes=64)
+        nc.sync.dma_start(old_sb[:], old.rearrange("(i p) n -> p i n", p=P))
+
+        w_codes = sb.tile([P, N], U32, name="w_codes", align_bytes=64)
+        w_scale = sb.tile([P, N], U8, name="w_scale", align_bytes=64)
+
+        def quantize_w(c0, c1):
+            h = c0 // HALF
+            grouped = sb.tile([P, PACK * (c1 - c0)], BF16, name="w_grouped%d" % c0, align_bytes=64)
+            dst, src = interleave_views(grouped[:], w_raw[h][:, :, c0 - h * HALF : c1 - h * HALF])
+            nc.scalar.copy(dst, src)
+            nc.vector.quantize_mx(w_codes[:, c0:c1].bitcast(FP8X4), w_scale[:, c0:c1], grouped[:])
+
+        def first_product(dst, s, c0, c1):
+            nc.tensor.matmul_mx(
+                dst,
+                lhsT=x_codes[:, s * P : (s + 1) * P].bitcast(FP8X4),
+                lhsT_scale=x_scale[:, s * P : (s + 1) * P],
+                rhs=w_codes[:, c0:c1].bitcast(FP8X4),
+                rhs_scale=w_scale[:, c0:c1],
+                start=True,
+                stop=True,
+            )
+
+        codes = {}
+        scale = {}
+        for o in (A, VV):
+            for g in range(PASSES):
+                codes[o, g] = sb.tile([P, N], U32, name="codes%d%d" % (o, g), align_bytes=64)
+                scale[o, g] = sb.tile([P, N], U8, name="scale%d%d" % (o, g), align_bytes=64)
+
+        def quantize(o, g, c0, c1, grouped):
+            nc.vector.quantize_mx(codes[o, g][:, c0:c1].bitcast(FP8X4), scale[o, g][:, c0:c1], grouped)
+
+        y_quads = []
+        for c in range(2):
+            quantize_w(c * P, (c + 1) * P)
+            y_quad = bank(c, "y_quad%d" % c)
+            for j in range(PACK):
+                first_product(y_quad[:, j * P : (j + 1) * P], j, c * P, (c + 1) * P)
+            y_quads.append(y_quad)
+
+        y_pairs = {}
+
+        def pair_products(g, h, first_bank):
+            for u in range(2):
+                y_pair = bank(first_bank + u, "y_pair%d%d%d" % (g, h, u))
+                for e in range(2):
+                    first_product(
+                        y_pair[:, e * HALF : (e + 1) * HALF],
+                        PACK * g + 2 * u + e,
+                        h * HALF,
+                        (h + 1) * HALF,
+                    )
+                y_pairs[g, h, u] = y_pair
+
+        pair_products(1, 0, 2)
+        quantize_w(HALF, N)
+        pair_products(0, 1, 4)
+        pair_products(1, 1, 6)
+
+        direct = {}
+        for o in (VV, A):
+            direct[o] = sb.tile([P, PACK * HALF], BF16, name="direct%d" % o, align_bytes=64)
+        for c in range(2):
+            for o in (VV, A):
+                nc.vector.tensor_tensor(
+                    direct[o][:, c * PACK * P : (c + 1) * PACK * P].rearrange("p (n j) -> p n j", j=PACK),
+                    y_quads[c][:].rearrange("p (j n) -> p n j", j=PACK),
+                    coef[:, o * SLOTS : o * SLOTS + PACK].unsqueeze(1).to_broadcast([P, P, PACK]),
+                    MULT,
+                )
+        for o in (VV, A):
+            quantize(o, 0, 0, HALF, direct[o][:])
+
+        def scaled_planes(o, g, c0, c1):
+            h = c0 // HALF
+            planes = sb.tile([P, PACK, c1 - c0], BF16, name="planes%d%d_%d" % (o, g, c0), align_bytes=64)
+            for j in range(PACK):
+                first = (j % 2 - h) * HALF
+                col = o * SLOTS + PACK * g + j
+                nc.scalar.activation(
+                    planes[:, j, :],
+                    y_pairs[g, h, j // 2][:, first + c0 : first + c1],
+                    COPY,
+                    scale=coef[:, col : col + 1],
+                )
+            grouped = sb.tile([P, PACK * (c1 - c0)], BF16, name="grouped%d%d_%d" % (o, g, c0), align_bytes=64)
+            dst, src = interleave_views(grouped[:], planes[:])
+            nc.vector.tensor_copy(dst, src)
+            quantize(o, g, c0, c1, grouped[:])
+
+        acc = {}
+
+        def second_product(i, g):
+            if g == 0:
+                acc[i] = bank(i, "acc%d" % i)
+            nc.tensor.matmul_mx(
+                acc[i][:],
+                lhsT=codes[A, g][:, i * P : (i + 1) * P].bitcast(FP8X4),
+                lhsT_scale=scale[A, g][:, i * P : (i + 1) * P],
+                rhs=codes[VV, g][:].bitcast(FP8X4),
+                rhs_scale=scale[VV, g][:],
+                start=(g == 0),
+                stop=(g == PASSES - 1),
+            )
+
+        kept = {}
+
+        def scale_old(i):
+            kept[i] = sb.tile([P, N], F32, name="kept%d" % i, align_bytes=64)
+            nc.scalar.activation(kept[i][:], old_sb[:, i, :], COPY, scale=KEEP)
+
+        def finish(i):
+            result = sb.tile([P, N], F32, name="result%d" % i, align_bytes=64)
+            nc.vector.scalar_tensor_tensor(result[:], acc[i][:], GAIN, kept[i][:], MULT, ADD)
+            nc.sync.dma_start(out[i * P : (i + 1) * P, :], result[:])
+
+        scaled_planes(VV, 1, 0, HALF)
+        scaled_planes(A, 1, 0, HALF)
+        scaled_planes(VV, 0, HALF, N)
+        scaled_planes(VV, 1, HALF, N)
+        for i in range(2):
+            for g in range(PASSES):
+                second_product(i, g)
+        scaled_planes(A, 0, HALF, N)
+        second_product(2, 0)
+        second_product(3, 0)
+        scale_old(0)
+        for i in (2, 3):
+            scaled_planes(A, 1, i * P, (i + 1) * P)
+            second_product(i, 1)
+        finish(0)
+        for i in (1, 2, 3):
+            scale_old(i)
+            finish(i)

@@ -48,38 +48,37 @@ def tile_picked_ykfac_lin_p_kernel(
 
         offsets = sb.tile([P, S // 16], U16, name="offsets")
         nc.sync.dma_start(offsets[:], offs)
-        word_table = sb.tile([P, T], U32, name="word_table", tag="table", align_bytes=64)
+        scale_table = sb.tile([P, T], U8, name="scale_table", align_bytes=64)
+        nc.sync.dma_start(scale_table[LAST16:P, :].bitcast(I32), x_scales[0].bitcast(I32))
+        coef_rows = sb.tile([P, P], F32, name="coef_rows", align_bytes=64)
+        for o, vec in ((A, wgt), (VV, inv)):
+            nc.sync.dma_start(
+                coef_rows[LAST16 + o * SLOTS : LAST16 + (o + 1) * SLOTS, :].rearrange("s (q r) -> s q r", r=RUN),
+                vec.rearrange("(q s r) o -> s q (r o)", s=SLOTS, r=RUN),
+            )
+        word_table = sb.tile([P, T], U32, name="word_table", align_bytes=64)
         nc.sync.dma_start(
             word_table[:].bitcast(I32), x_words[0].rearrange("p n t -> p (n t)").bitcast(I32)
         )
         w_rows = w1.rearrange("(p j) n -> p j n", j=PACK)
-        w_raw = []
-        for h in range(2):
-            w_half = sb.tile([P, PACK, HALF], F32, name="w_raw%d" % h, align_bytes=64)
-            nc.sync.dma_start(w_half[:], w_rows[:, :, h * HALF : (h + 1) * HALF])
-            w_raw.append(w_half)
+        w_first = sb.tile([P, PACK, HALF], F32, name="w_first", align_bytes=64)
+        nc.sync.dma_start(w_first[:], w_rows[:, :, 0:HALF])
 
-        scale_table = sb.tile([P, T], U8, name="scale_table", align_bytes=64)
-        nc.scalar.dma_start(scale_table[LAST16:P, :].bitcast(I32), x_scales[0].bitcast(I32))
+        zeros = sb.tile([P, P], F32, name="zeros", align_bytes=64)
+        nc.vector.memset(zeros[:], 0.0)
         nc.vector.memset(scale_table[0:LAST16, :].bitcast(I32), 0)
 
-        coef_rows = sb.tile([P, P], F32, name="coef_rows", align_bytes=64)
-        for o, vec in ((A, wgt), (VV, inv)):
-            nc.scalar.dma_start(
-                coef_rows[LAST16 + o * SLOTS : LAST16 + (o + 1) * SLOTS, :].rearrange("s (q r) -> s q r", r=RUN),
-                vec.rearrange("(q s r) o -> s q (r o)", s=SLOTS, r=RUN),
-            )
+        nc.scalar.activation(coef_rows[0:LAST16, :], zeros[0:LAST16, :], COPY)
         x_scale = sb.tile([P, S], U8, name="x_scale", align_bytes=64)
         nc.gpsimd.memset(x_scale[:].bitcast(I32), 0)
         ident = sb.tile([P, P], F32, name="ident", align_bytes=64)
         make_identity(nc, ident[:])
-        nc.scalar.activation(coef_rows[0:LAST16, :], ident[0:LAST16, :], COPY)
         coef_ps = bank(7, "coef_ps", P)
         nc.tensor.transpose(coef_ps[:], coef_rows[:], ident[:])
         coef = sb.tile([P, 2 * SLOTS], F32, name="coef", align_bytes=64)
         nc.scalar.activation(coef[:], coef_ps[:, LAST16:P], COPY)
 
-        picked_scales = sb.tile([P, S], U8, name="picked_scales", align_bytes=64)
+        picked_scales = sb.tile([P, S], U8, name="picked_scales", tag="late", align_bytes=64)
         nc.vector.tensor_copy(picked_scales[:], scale_table[:].indirect(offsets[:]))
         dealt_scales = sb.tile([P, S], U8, name="dealt_scales", align_bytes=64)
         nc.vector.tensor_copy(
@@ -87,19 +86,25 @@ def tile_picked_ykfac_lin_p_kernel(
             picked_scales[:].bitcast(I32).rearrange("p (q s w) -> p s q w", s=SLOTS, w=RUN // 4),
         )
         for quad in range(4):
-            nc.scalar.dma_start(
+            nc.sync.dma_start(
                 x_scale[32 * quad : 32 * quad + 4, :].bitcast(I32),
                 dealt_scales[LAST16 + 4 * quad : LAST16 + 4 * (quad + 1), :].bitcast(I32),
             )
+
+        late = sb.tile([P, PACK * HALF + (N // P) * N], F32, name="late", tag="late", align_bytes=64)
+        w_second = late[:, 0 : PACK * HALF].rearrange("p (j n) -> p j n", j=PACK)
+        nc.sync.dma_start(w_second, w_rows[:, :, HALF:N])
+        w_raw = [w_first[:], w_second]
+        old_sb = late[:, PACK * HALF :].rearrange("p (i n) -> p i n", n=N)
+        old_rows = old.rearrange("(i p) n -> p i n", p=P)
+        for u in range(2):
+            nc.sync.dma_start(old_sb[:, 2 * u : 2 * u + 2, :], old_rows[:, 2 * u : 2 * u + 2, :])
 
         x_codes = sb.tile([P, S], U32, name="x_codes", align_bytes=64)
         nc.vector.tensor_copy(
             x_codes[:].rearrange("p (s q r) -> p q s r", s=SLOTS, r=RUN),
             word_table[:].indirect(offsets[:]),
         )
-
-        old_sb = sb.tile([P, N // P, N], F32, name="old_sb", tag="table", align_bytes=64)
-        nc.sync.dma_start(old_sb[:], old.rearrange("(i p) n -> p i n", p=P))
 
         w_codes = sb.tile([P, N], U32, name="w_codes", align_bytes=64)
         w_scale = sb.tile([P, N], U8, name="w_scale", align_bytes=64)
@@ -122,85 +127,101 @@ def tile_picked_ykfac_lin_p_kernel(
                 stop=True,
             )
 
-        codes = {}
-        scale = {}
-        for o in (A, VV):
-            for g in range(PASSES):
-                codes[o, g] = sb.tile([P, N], U32, name="codes%d%d" % (o, g), align_bytes=64)
-                scale[o, g] = sb.tile([P, N], U8, name="scale%d%d" % (o, g), align_bytes=64)
+        codes = [sb.tile([P, 2 * N], U32, name="codes%d" % g, align_bytes=64) for g in range(PASSES)]
+        scale = [sb.tile([P, 2 * N], U8, name="scale%d" % g, align_bytes=64) for g in range(PASSES)]
 
-        def quantize(o, g, c0, c1, grouped):
-            nc.vector.quantize_mx(codes[o, g][:, c0:c1].bitcast(FP8X4), scale[o, g][:, c0:c1], grouped)
+        def place(o, c):
+            if o == VV:
+                return HALF + c
+            return c if c < HALF else N + c
 
-        y_quads = []
-        for c in range(2):
-            quantize_w(c * P, (c + 1) * P)
-            y_quad = bank(c, "y_quad%d" % c)
-            for j in range(PACK):
-                first_product(y_quad[:, j * P : (j + 1) * P], j, c * P, (c + 1) * P)
-            y_quads.append(y_quad)
+        def quantize(g, first, width, grouped):
+            cols = slice(first, first + width)
+            nc.vector.quantize_mx(codes[g][:, cols].bitcast(FP8X4), scale[g][:, cols], grouped)
 
+        y_quads = {}
         y_pairs = {}
 
-        def pair_products(g, h, first_bank):
-            for u in range(2):
-                y_pair = bank(first_bank + u, "y_pair%d%d%d" % (g, h, u))
-                for e in range(2):
-                    first_product(
-                        y_pair[:, e * HALF : (e + 1) * HALF],
-                        PACK * g + 2 * u + e,
-                        h * HALF,
-                        (h + 1) * HALF,
-                    )
-                y_pairs[g, h, u] = y_pair
-
-        pair_products(1, 0, 2)
-        quantize_w(HALF, N)
-        pair_products(0, 1, 4)
-        pair_products(1, 1, 6)
-
-        direct = {}
-        for o in (VV, A):
-            direct[o] = sb.tile([P, PACK * HALF], BF16, name="direct%d" % o, align_bytes=64)
-        for c in range(2):
-            for o in (VV, A):
-                nc.vector.tensor_tensor(
-                    direct[o][:, c * PACK * P : (c + 1) * PACK * P].rearrange("p (n j) -> p n j", j=PACK),
-                    y_quads[c][:].rearrange("p (j n) -> p n j", j=PACK),
-                    coef[:, o * SLOTS : o * SLOTS + PACK].unsqueeze(1).to_broadcast([P, P, PACK]),
-                    MULT,
-                )
-        for o in (VV, A):
-            quantize(o, 0, 0, HALF, direct[o][:])
-
-        def scaled_planes(o, g, c0, c1):
-            h = c0 // HALF
-            planes = sb.tile([P, PACK, c1 - c0], BF16, name="planes%d%d_%d" % (o, g, c0), align_bytes=64)
+        def quad_products(c):
+            y_quads[c] = bank(c, "y_quad%d" % c)
             for j in range(PACK):
+                first_product(y_quads[c][:, j * P : (j + 1) * P], j, c * P, (c + 1) * P)
+
+        def pair_products(g, h, u, b):
+            y_pairs[g, h, u] = bank(b, "y_pair%d%d%d" % (g, h, u))
+            for e in range(2):
+                first_product(
+                    y_pairs[g, h, u][:, e * HALF : (e + 1) * HALF],
+                    PACK * g + 2 * u + e,
+                    h * HALF,
+                    (h + 1) * HALF,
+                )
+
+        quantize_w(0, P)
+        quantize_w(P, HALF)
+        for c in range(2):
+            quad_products(c)
+            pair_products(1, 0, c, 2 + c)
+        quantize_w(HALF, N)
+        for g in range(PASSES):
+            for u in range(2):
+                pair_products(g, 1, u, 4 + 2 * g + u)
+
+        direct = sb.tile([P, 2 * PACK * HALF], BF16, name="direct", align_bytes=64)
+        direct_view = direct[:].rearrange("p (o n j) -> p o n j", o=2, j=PACK)
+        factors = coef[:].rearrange("p (o s) -> p o s", o=2)[:, :, 0:PACK]
+        for c in range(2):
+            nc.vector.tensor_tensor(
+                direct_view[:, :, c * P : (c + 1) * P, :],
+                y_quads[c][:].rearrange("p (j n) -> p n j", j=PACK).unsqueeze(1).to_broadcast([P, 2, P, PACK]),
+                factors.unsqueeze(2).to_broadcast([P, 2, P, PACK]),
+                MULT,
+            )
+        quantize(0, 0, N, direct[:])
+
+        planes = {}
+
+        def scale_planes(o, g, c0, c1, slots):
+            h = c0 // HALF
+            if (o, g, c0) not in planes:
+                planes[o, g, c0] = sb.tile(
+                    [P, PACK, c1 - c0], BF16, name="planes%d%d_%d" % (o, g, c0), align_bytes=64
+                )
+            for j in slots:
                 first = (j % 2 - h) * HALF
                 col = o * SLOTS + PACK * g + j
                 nc.scalar.activation(
-                    planes[:, j, :],
+                    planes[o, g, c0][:, j, :],
                     y_pairs[g, h, j // 2][:, first + c0 : first + c1],
                     COPY,
                     scale=coef[:, col : col + 1],
                 )
-            grouped = sb.tile([P, PACK * (c1 - c0)], BF16, name="grouped%d%d_%d" % (o, g, c0), align_bytes=64)
-            dst, src = interleave_views(grouped[:], planes[:])
+
+        grouped = {}
+
+        def interleave(o, g, c0, c1):
+            grouped[o, g, c0] = sb.tile(
+                [P, PACK * (c1 - c0)], BF16, name="grouped%d%d_%d" % (o, g, c0), align_bytes=64
+            )
+            dst, src = interleave_views(grouped[o, g, c0][:], planes[o, g, c0][:])
             nc.vector.tensor_copy(dst, src)
-            quantize(o, g, c0, c1, grouped[:])
+
+        def quantize_group(o, g, c0, c1):
+            quantize(g, place(o, c0), c1 - c0, grouped[o, g, c0][:])
 
         acc = {}
 
         def second_product(i, g):
             if g == 0:
                 acc[i] = bank(i, "acc%d" % i)
+            a_cols = slice(place(A, i * P), place(A, i * P) + P)
+            vv_cols = slice(place(VV, 0), place(VV, 0) + N)
             nc.tensor.matmul_mx(
                 acc[i][:],
-                lhsT=codes[A, g][:, i * P : (i + 1) * P].bitcast(FP8X4),
-                lhsT_scale=scale[A, g][:, i * P : (i + 1) * P],
-                rhs=codes[VV, g][:].bitcast(FP8X4),
-                rhs_scale=scale[VV, g][:],
+                lhsT=codes[g][:, a_cols].bitcast(FP8X4),
+                lhsT_scale=scale[g][:, a_cols],
+                rhs=codes[g][:, vv_cols].bitcast(FP8X4),
+                rhs_scale=scale[g][:, vv_cols],
                 start=(g == 0),
                 stop=(g == PASSES - 1),
             )
@@ -216,20 +237,37 @@ def tile_picked_ykfac_lin_p_kernel(
             nc.vector.scalar_tensor_tensor(result[:], acc[i][:], GAIN, kept[i][:], MULT, ADD)
             nc.sync.dma_start(out[i * P : (i + 1) * P, :], result[:])
 
-        scaled_planes(VV, 1, 0, HALF)
-        scaled_planes(A, 1, 0, HALF)
-        scaled_planes(VV, 0, HALF, N)
-        scaled_planes(VV, 1, HALF, N)
-        for i in range(2):
-            for g in range(PASSES):
-                second_product(i, g)
-        scaled_planes(A, 0, HALF, N)
-        second_product(2, 0)
-        second_product(3, 0)
-        scale_old(0)
-        for i in (2, 3):
-            scaled_planes(A, 1, i * P, (i + 1) * P)
-            second_product(i, 1)
+        for slots in ((0, 1), (2, 3)):
+            for o in (VV, A):
+                scale_planes(o, 1, 0, HALF, slots)
+        groups = [
+            (VV, 1, 0, HALF),
+            (A, 1, 0, HALF),
+            (VV, 0, HALF, N),
+            (VV, 1, HALF, N),
+            (A, 0, HALF, N),
+            (A, 1, 2 * P, 3 * P),
+            (A, 1, 3 * P, 4 * P),
+        ]
+        for n, group in enumerate(groups):
+            if n == 5:
+                scale_old(0)
+            if n >= 2:
+                scale_planes(*group, range(PACK))
+            interleave(*group)
+            if n >= 1:
+                quantize_group(*groups[n - 1])
+            if n == 4:
+                for i in range(2):
+                    for g in range(PASSES):
+                        second_product(i, g)
+            if n == 5:
+                second_product(2, 0)
+                second_product(3, 0)
+            if n == 6:
+                second_product(2, 1)
+        quantize_group(*groups[-1])
+        second_product(3, 1)
         finish(0)
         for i in (1, 2, 3):
             scale_old(i)

@@ -80,7 +80,7 @@ def tile_picked_ykfac_lin_p_kernel(
 
         picked_scales = sb.tile([P, S], U8, name="picked_scales", tag="late", align_bytes=64)
         nc.vector.tensor_copy(picked_scales[:], scale_table[:].indirect(offsets[:]))
-        dealt_scales = sb.tile([P, S], U8, name="dealt_scales", align_bytes=64)
+        dealt_scales = sb.tile([P, S], U8, name="dealt_scales", tag="later", align_bytes=64)
         nc.vector.tensor_copy(
             dealt_scales[:].bitcast(I32).rearrange("p (s q w) -> p s q w", s=SLOTS, w=RUN // 4),
             picked_scales[:].bitcast(I32).rearrange("p (q s w) -> p s q w", s=SLOTS, w=RUN // 4),
@@ -91,12 +91,11 @@ def tile_picked_ykfac_lin_p_kernel(
                 dealt_scales[LAST16 + 4 * quad : LAST16 + 4 * (quad + 1), :].bitcast(I32),
             )
 
-        late = sb.tile([P, PACK * HALF + (N // P) * N], F32, name="late", tag="late", align_bytes=64)
-        w_second = late[:, 0 : PACK * HALF].rearrange("p (j n) -> p j n", j=PACK)
-        nc.sync.dma_start(w_second, w_rows[:, :, HALF:N])
-        w_raw = [w_first[:], w_second]
-        old_sb = late[:, PACK * HALF :].rearrange("p (i n) -> p i n", n=N)
+        w_second = sb.tile([P, PACK, HALF], F32, name="w_second", tag="late", align_bytes=64)
+        nc.sync.dma_start(w_second[:], w_rows[:, :, HALF:N])
+        w_raw = [w_first[:], w_second[:]]
         old_rows = old.rearrange("(i p) n -> p i n", p=P)
+        old_sb = sb.tile([P, N // P, N], F32, name="old_sb", tag="later", align_bytes=64)
         for u in range(2):
             nc.sync.dma_start(old_sb[:, 2 * u : 2 * u + 2, :], old_rows[:, 2 * u : 2 * u + 2, :])
 
@@ -109,9 +108,14 @@ def tile_picked_ykfac_lin_p_kernel(
         w_codes = sb.tile([P, N], U32, name="w_codes", align_bytes=64)
         w_scale = sb.tile([P, N], U8, name="w_scale", align_bytes=64)
 
+        direct = sb.tile([P, 2 * PACK * HALF], BF16, name="direct", align_bytes=64)
+
         def quantize_w(c0, c1):
             h = c0 // HALF
-            grouped = sb.tile([P, PACK * (c1 - c0)], BF16, name="w_grouped%d" % c0, align_bytes=64)
+            if c0 == 2 * P:
+                grouped = direct[:, PACK * P : 2 * PACK * P]
+            else:
+                grouped = sb.tile([P, PACK * P], BF16, name="w_grouped%d" % c0, tag="w_grouped%d" % c0, align_bytes=64)
             dst, src = interleave_views(grouped[:], w_raw[h][:, :, c0 - h * HALF : c1 - h * HALF])
             nc.scalar.copy(dst, src)
             nc.vector.quantize_mx(w_codes[:, c0:c1].bitcast(FP8X4), w_scale[:, c0:c1], grouped[:])
@@ -162,14 +166,14 @@ def tile_picked_ykfac_lin_p_kernel(
         for c in range(2):
             quad_products(c)
             pair_products(1, 0, c, 2 + c)
-        quantize_w(HALF, N)
+        quantize_w(3 * P, N)
+        quantize_w(2 * P, 3 * P)
         for g in range(PASSES):
             for u in range(2):
                 pair_products(g, 1, u, 4 + 2 * g + u)
 
-        direct = sb.tile([P, 2 * PACK * HALF], BF16, name="direct", align_bytes=64)
-        direct_view = direct[:].rearrange("p (o n j) -> p o n j", o=2, j=PACK)
         factors = coef[:].rearrange("p (o s) -> p o s", o=2)[:, :, 0:PACK]
+        direct_view = direct[:].rearrange("p (o n j) -> p o n j", o=2, j=PACK)
         for c in range(2):
             nc.vector.tensor_tensor(
                 direct_view[:, :, c * P : (c + 1) * P, :],
@@ -179,7 +183,8 @@ def tile_picked_ykfac_lin_p_kernel(
             )
         quantize(0, 0, N, direct[:])
 
-        planes = {}
+        first_planes = sb.tile([P, 2, PACK, HALF], BF16, name="first_planes", tag="late", align_bytes=64)
+        planes = {(o, 1, 0): first_planes[:, o] for o in (A, VV)}
 
         def scale_planes(o, g, c0, c1, slots):
             h = c0 // HALF
@@ -199,12 +204,15 @@ def tile_picked_ykfac_lin_p_kernel(
 
         grouped = {}
 
-        def interleave(o, g, c0, c1):
+        def interleave(o, g, c0, c1, on_scalar=False):
             grouped[o, g, c0] = sb.tile(
-                [P, PACK * (c1 - c0)], BF16, name="grouped%d%d_%d" % (o, g, c0), align_bytes=64
+                [P, PACK * (c1 - c0)], BF16, name="grouped%d%d_%d" % (o, g, c0), tag="grouped%d%d_%d" % (o, g, c0), align_bytes=64
             )
-            dst, src = interleave_views(grouped[o, g, c0][:], planes[o, g, c0][:])
-            nc.vector.tensor_copy(dst, src)
+            dst, src = interleave_views(grouped[o, g, c0][:], planes[o, g, c0][:, :, :])
+            if on_scalar:
+                nc.scalar.copy(dst, src)
+            else:
+                nc.vector.tensor_copy(dst, src)
 
         def quantize_group(o, g, c0, c1):
             quantize(g, place(o, c0), c1 - c0, grouped[o, g, c0][:])
@@ -232,43 +240,63 @@ def tile_picked_ykfac_lin_p_kernel(
             kept[i] = sb.tile([P, N], F32, name="kept%d" % i, align_bytes=64)
             nc.scalar.activation(kept[i][:], old_sb[:, i, :], COPY, scale=KEEP)
 
-        def finish(i):
-            result = sb.tile([P, N], F32, name="result%d" % i, align_bytes=64)
-            nc.vector.scalar_tensor_tensor(result[:], acc[i][:], GAIN, kept[i][:], MULT, ADD)
+        def finish_aside(i):
+            gained = sb.tile([P, N], F32, name="gained%d" % i, align_bytes=64)
+            nc.scalar.activation(gained[:], acc[i][:], COPY, scale=GAIN)
+            result = sb.tile([P, N], F32, name="result%d" % i, tag="grouped%d%d_%d" % (A, 1, 3 * P), align_bytes=64)
+            nc.gpsimd.tensor_tensor(result[:], gained[:], kept[i], ADD)
             nc.sync.dma_start(out[i * P : (i + 1) * P, :], result[:])
 
+        def finish(i, c0=0, c1=N):
+            result = sb.tile([P, c1 - c0], F32, name="result%d_%d" % (i, c0), align_bytes=64)
+            nc.vector.scalar_tensor_tensor(result[:], acc[i][:, c0:c1], GAIN, kept[i][:, c0:c1], MULT, ADD)
+            nc.sync.dma_start(out[i * P : (i + 1) * P, c0:c1], result[:])
+
+        kept01 = sb.tile([P, 2 * N], F32, name="kept01", tag="w_grouped%d" % (3 * P), align_bytes=64)
+        nc.gpsimd.tensor_scalar(kept01[:], old_sb[:, 0:2, :].rearrange("p i n -> p (i n)"), KEEP, 0.0, MULT, ADD)
+        kept[0] = kept01[:, 0:N]
+        kept[1] = kept01[:, N : 2 * N]
         for slots in ((0, 1), (2, 3)):
             for o in (VV, A):
                 scale_planes(o, 1, 0, HALF, slots)
-        groups = [
-            (VV, 1, 0, HALF),
-            (A, 1, 0, HALF),
-            (VV, 0, HALF, N),
-            (VV, 1, HALF, N),
-            (A, 0, HALF, N),
-            (A, 1, 2 * P, 3 * P),
-            (A, 1, 3 * P, 4 * P),
-        ]
-        for n, group in enumerate(groups):
-            if n == 5:
-                scale_old(0)
-            if n >= 2:
-                scale_planes(*group, range(PACK))
-            interleave(*group)
-            if n >= 1:
-                quantize_group(*groups[n - 1])
-            if n == 4:
-                for i in range(2):
-                    for g in range(PASSES):
-                        second_product(i, g)
-            if n == 5:
-                second_product(2, 0)
-                second_product(3, 0)
-            if n == 6:
-                second_product(2, 1)
-        quantize_group(*groups[-1])
+        g0 = (VV, 1, 0, HALF)
+        g1 = (A, 1, 0, HALF)
+        g2 = (VV, 0, HALF, N)
+        g3 = (VV, 1, HALF, N)
+        g4 = (A, 0, HALF, N)
+        g5 = (A, 1, 2 * P, 3 * P)
+        g6 = (A, 1, 3 * P, 4 * P)
+        interleave(*g0)
+        interleave(*g1)
+        quantize_group(*g0)
+        scale_planes(*g2, range(PACK))
+        interleave(*g2)
+        quantize_group(*g1)
+        scale_planes(*g3, range(PACK))
+        interleave(*g3)
+        quantize_group(*g2)
+        scale_planes(*g4, range(PACK))
+        interleave(*g4)
+        quantize_group(*g3)
+        second_product(0, 0)
+        second_product(0, 1)
+        second_product(1, 0)
+        second_product(1, 1)
+        scale_planes(*g5, range(PACK))
+        interleave(*g5)
+        quantize_group(*g4)
+        second_product(2, 0)
+        second_product(3, 0)
+        scale_planes(*g6, range(PACK))
+        interleave(*g6)
+        quantize_group(*g5)
+        second_product(2, 1)
+        quantize_group(*g6)
         second_product(3, 1)
+        finish_aside(1)
         finish(0)
-        for i in (1, 2, 3):
-            scale_old(i)
-            finish(i)
+        scale_old(2)
+        finish(2)
+        scale_old(3)
+        finish(3, 0, HALF)
+        finish(3, HALF, N)

@@ -116,8 +116,16 @@ def tile_picked_ykfac_lin_p_kernel(
                 grouped = direct[:, PACK * P : 2 * PACK * P]
             else:
                 grouped = sb.tile([P, PACK * P], BF16, name="w_grouped%d" % c0, tag="w_grouped%d" % c0, align_bytes=64)
-            dst, src = interleave_views(grouped[:], w_raw[h][:, :, c0 - h * HALF : c1 - h * HALF])
-            nc.scalar.copy(dst, src)
+            raw = w_raw[h][:, :, c0 - h * HALF : c1 - h * HALF]
+            if c0 == 2 * P:
+                nc.gpsimd.tensor_scalar(
+                    grouped.rearrange("p (n j) -> p n j", j=PACK),
+                    raw.rearrange("p j n -> p n j"),
+                    1.0, 0.0, MULT, ADD,
+                )
+            else:
+                dst, src = interleave_views(grouped[:], raw)
+                nc.scalar.copy(dst, src)
             nc.vector.quantize_mx(w_codes[:, c0:c1].bitcast(FP8X4), w_scale[:, c0:c1], grouped[:])
 
         def first_product(dst, s, c0, c1):

@@ -52,7 +52,7 @@ def tile_picked_ykfac_lin_p_kernel(
         nc.sync.dma_start(scale_table[LAST16:P, :].bitcast(I32), x_scales[0].bitcast(I32))
         coef_rows = sb.tile([P, P], F32, name="coef_rows", align_bytes=64)
         for o, vec in ((A, wgt), (VV, inv)):
-            nc.sync.dma_start(
+            nc.scalar.dma_start(
                 coef_rows[LAST16 + o * SLOTS : LAST16 + (o + 1) * SLOTS, :].rearrange("s (q r) -> s q r", r=RUN),
                 vec.rearrange("(q s r) o -> s q (r o)", s=SLOTS, r=RUN),
             )
@@ -113,7 +113,7 @@ def tile_picked_ykfac_lin_p_kernel(
         def quantize_w(c0, c1):
             h = c0 // HALF
             if c0 == 2 * P:
-                grouped = direct[:, PACK * P : 2 * PACK * P]
+                grouped = direct[:, 3 * PACK * P : 4 * PACK * P]
             else:
                 grouped = sb.tile([P, PACK * P], BF16, name="w_grouped%d" % c0, tag="w_grouped%d" % c0, align_bytes=64)
             raw = w_raw[h][:, :, c0 - h * HALF : c1 - h * HALF]
@@ -180,15 +180,15 @@ def tile_picked_ykfac_lin_p_kernel(
             for u in range(2):
                 pair_products(g, 1, u, 4 + 2 * g + u)
 
-        factors = coef[:].rearrange("p (o s) -> p o s", o=2)[:, :, 0:PACK]
-        direct_view = direct[:].rearrange("p (o n j) -> p o n j", o=2, j=PACK)
         for c in range(2):
-            nc.vector.tensor_tensor(
-                direct_view[:, :, c * P : (c + 1) * P, :],
-                y_quads[c][:].rearrange("p (j n) -> p n j", j=PACK).unsqueeze(1).to_broadcast([P, 2, P, PACK]),
-                factors.unsqueeze(2).to_broadcast([P, 2, P, PACK]),
-                MULT,
-            )
+            for o in (VV, A):
+                first = PACK * (o * HALF + c * P)
+                nc.vector.tensor_tensor(
+                    direct[:, first : first + PACK * P].rearrange("p (n i j) -> p n j i", i=2, j=PACK),
+                    y_quads[c][:].rearrange("p (j n i) -> p n j i", i=2, j=PACK),
+                    coef[:, o * SLOTS : o * SLOTS + PACK].unsqueeze(1).unsqueeze(3).to_broadcast([P, P // 2, PACK, 2]),
+                    MULT,
+                )
         quantize(0, 0, N, direct[:])
 
         first_planes = sb.tile([P, 2, PACK, HALF], BF16, name="first_planes", tag="late", align_bytes=64)

from contextlib import ExitStack

import concourse.mybir as mybir
from concourse.masks import make_identity

K, T, S, N = 512, 4096, 1024, 512
FLOPS = 2 * S * K * N + 2 * S * N * N

F32 = mybir.dt.float32
BF16 = mybir.dt.bfloat16
I32 = mybir.dt.int32
U32 = mybir.dt.uint32
U16 = mybir.dt.uint16
U8 = mybir.dt.uint8
FP8X4 = mybir.dt.float8_e4m3fn_x4
COPY = mybir.ActivationFunctionType.Copy
MULT = mybir.AluOpType.mult
ADD = mybir.AluOpType.add

P = 128
PACK = 4
PASSES = S // (P * PACK)
SLOTS = PASSES * PACK
RUN = 8
HALF = N // 2
KEEP, GAIN = 0.95, 0.05
A, VV = 0, 1
LAST16 = P - 16


def interleave_views(grouped, planes):
    return (
        grouped.rearrange("p (c i t) -> p c t i", i=4, t=PACK),
        planes.rearrange("p t (c i) -> p c t i", i=4),
    )


def tile_picked_ykfac_lin_p_kernel(
    tc, x_words, x_scales, w1, wgt, inv, old, offs, out
):
    nc = tc.nc
    with ExitStack() as ctx:
        sb = ctx.enter_context(tc.tile_pool(name="sb", bufs=1))
        ps = ctx.enter_context(tc.psum_pool(name="ps", bufs=1))

        def bank(b, name, cols=N):
            return ps.tile([P, cols], F32, name=name, tag="bank%d" % b)

        offsets = sb.tile([P, S // 16], U16, name="offsets")
        nc.sync.dma_start(offsets[:], offs)
        scale_table = sb.tile([P, T], U8, name="scale_table", align_bytes=64)
        nc.sync.dma_start(scale_table[LAST16:P, :].bitcast(I32), x_scales[0].bitcast(I32))
        coef_rows = sb.tile([P, P], F32, name="coef_rows", align_bytes=64)
        for o, vec in ((A, wgt), (VV, inv)):
            nc.scalar.dma_start(
                coef_rows[LAST16 + o * SLOTS : LAST16 + (o + 1) * SLOTS, :].rearrange("s (q r) -> s q r", r=RUN),
                vec.rearrange("(q s r) o -> s q (r o)", s=SLOTS, r=RUN),
            )
        word_table = sb.tile([P, T], U32, name="word_table", align_bytes=64)
        nc.sync.dma_start(
            word_table[:].bitcast(I32), x_words[0].rearrange("p n t -> p (n t)").bitcast(I32)
        )
        w_rows = w1.rearrange("(p j) n -> p j n", j=PACK)
        w_first = sb.tile([P, PACK, HALF], F32, name="w_first", align_bytes=64)
        nc.sync.dma_start(w_first[:], w_rows[:, :, 0:HALF])

        zeros = sb.tile([P, P], F32, name="zeros", align_bytes=64)
        nc.vector.memset(zeros[:], 0.0)
        nc.vector.memset(scale_table[0:LAST16, :].bitcast(I32), 0)

        nc.scalar.activation(coef_rows[0:LAST16, :], zeros[0:LAST16, :], COPY)
        x_scale = sb.tile([P, S], U8, name="x_scale", align_bytes=64)
        nc.gpsimd.memset(x_scale[:].bitcast(I32), 0)
        ident = sb.tile([P, P], F32, name="ident", align_bytes=64)
        make_identity(nc, ident[:])
        coef_ps = bank(7, "coef_ps", P)
        nc.tensor.transpose(coef_ps[:], coef_rows[:], ident[:])
        coef = sb.tile([P, 2 * SLOTS], F32, name="coef", align_bytes=64)
        nc.scalar.activation(coef[:], coef_ps[:, LAST16:P], COPY)

        picked_scales = sb.tile([P, S], U8, name="picked_scales", tag="late", align_bytes=64)
        nc.vector.tensor_copy(picked_scales[:], scale_table[:].indirect(offsets[:]))
        dealt_scales = sb.tile([P, S], U8, name="dealt_scales", tag="later", align_bytes=64)
        nc.vector.tensor_copy(
            dealt_scales[:].bitcast(I32).rearrange("p (s q w) -> p s q w", s=SLOTS, w=RUN // 4),
            picked_scales[:].bitcast(I32).rearrange("p (q s w) -> p s q w", s=SLOTS, w=RUN // 4),
        )
        for quad in range(4):
            nc.sync.dma_start(
                x_scale[32 * quad : 32 * quad + 4, :].bitcast(I32),
                dealt_scales[LAST16 + 4 * quad : LAST16 + 4 * (quad + 1), :].bitcast(I32),
            )

        w_second = sb.tile([P, PACK, HALF], F32, name="w_second", tag="late", align_bytes=64)
        nc.sync.dma_start(w_second[:], w_rows[:, :, HALF:N])
        w_raw = [w_first[:], w_second[:]]
        old_rows = old.rearrange("(i p) n -> p i n", p=P)
        old_sb = sb.tile([P, N // P, N], F32, name="old_sb", tag="later", align_bytes=64)
        for u in range(2):
            nc.sync.dma_start(old_sb[:, 2 * u : 2 * u + 2, :], old_rows[:, 2 * u : 2 * u + 2, :])

        x_codes = sb.tile([P, S], U32, name="x_codes", align_bytes=64)
        nc.vector.tensor_copy(
            x_codes[:].rearrange("p (s q r) -> p q s r", s=SLOTS, r=RUN),
            word_table[:].indirect(offsets[:]),
        )

        w_codes = sb.tile([P, N], U32, name="w_codes", align_bytes=64)
        w_scale = sb.tile([P, N], U8, name="w_scale", align_bytes=64)

        direct = sb.tile([P, 2 * PACK * HALF], BF16, name="direct", align_bytes=64)

        def quantize_w(c0, c1):
            h = c0 // HALF
            if c0 == 2 * P:
                grouped = direct[:, 3 * PACK * P : 4 * PACK * P]
            else:
                grouped = sb.tile([P, PACK * P], BF16, name="w_grouped%d" % c0, tag="w_grouped%d" % c0, align_bytes=64)
            raw = w_raw[h][:, :, c0 - h * HALF : c1 - h * HALF]
            if c0 == 2 * P:
                nc.gpsimd.tensor_scalar(
                    grouped.rearrange("p (n j) -> p n j", j=PACK),
                    raw.rearrange("p j n -> p n j"),
                    1.0, 0.0, MULT, ADD,
                )
            else:
                dst, src = interleave_views(grouped[:], raw)
                nc.scalar.copy(dst, src)
            nc.vector.quantize_mx(w_codes[:, c0:c1].bitcast(FP8X4), w_scale[:, c0:c1], grouped[:])

        def first_product(dst, s, c0, c1):
            nc.tensor.matmul_mx(
                dst,
                lhsT=x_codes[:, s * P : (s + 1) * P].bitcast(FP8X4),
                lhsT_scale=x_scale[:, s * P : (s + 1) * P],
                rhs=w_codes[:, c0:c1].bitcast(FP8X4),
                rhs_scale=w_scale[:, c0:c1],
                start=True,
                stop=True,
            )

        codes = [sb.tile([P, 2 * N], U32, name="codes%d" % g, align_bytes=64) for g in range(PASSES)]
        scale = [sb.tile([P, 2 * N], U8, name="scale%d" % g, align_bytes=64) for g in range(PASSES)]

        def place(o, c):
            if o == VV:
                return HALF + c
            return c if c < HALF else N + c

        def quantize(g, first, width, grouped):
            cols = slice(first, first + width)
            nc.vector.quantize_mx(codes[g][:, cols].bitcast(FP8X4), scale[g][:, cols], grouped)

        y_quads = {}
        y_pairs = {}

        def quad_products(c):
            y_quads[c] = bank(c, "y_quad%d" % c)
            for j in range(PACK):
                first_product(y_quads[c][:, j * P : (j + 1) * P], j, c * P, (c + 1) * P)

        def pair_products(g, h, u, b):
            y_pairs[g, h, u] = bank(b, "y_pair%d%d%d" % (g, h, u))
            for e in range(2):
                first_product(
                    y_pairs[g, h, u][:, e * HALF : (e + 1) * HALF],
                    PACK * g + 2 * u + e,
                    h * HALF,
                    (h + 1) * HALF,
                )

        quantize_w(0, P)
        quantize_w(P, HALF)
        for c in range(2):
            quad_products(c)
            pair_products(1, 0, c, 2 + c)
        quantize_w(3 * P, N)
        quantize_w(2 * P, 3 * P)
        for g in range(PASSES):
            for u in range(2):
                pair_products(g, 1, u, 4 + 2 * g + u)

        for c in range(2):
            for o in (VV, A):
                first = PACK * (o * HALF + c * P)
                nc.vector.tensor_tensor(
                    direct[:, first : first + PACK * P].rearrange("p (n i j) -> p n j i", i=2, j=PACK),
                    y_quads[c][:].rearrange("p (j n i) -> p n j i", i=2, j=PACK),
                    coef[:, o * SLOTS : o * SLOTS + PACK].unsqueeze(1).unsqueeze(3).to_broadcast([P, P // 2, PACK, 2]),
                    MULT,
                )
        quantize(0, 0, N, direct[:])

        first_planes = sb.tile([P, 2, PACK, HALF], BF16, name="first_planes", tag="late", align_bytes=64)
        planes = {(o, 1, 0): first_planes[:, o] for o in (A, VV)}

        def scale_planes(o, g, c0, c1, slots):
            h = c0 // HALF
            if (o, g, c0) not in planes:
                planes[o, g, c0] = sb.tile(
                    [P, PACK, c1 - c0], BF16, name="planes%d%d_%d" % (o, g, c0), align_bytes=64
                )
            for j in slots:
                first = (j % 2 - h) * HALF
                col = o * SLOTS + PACK * g + j
                nc.scalar.activation(
                    planes[o, g, c0][:, j, :],
                    y_pairs[g, h, j // 2][:, first + c0 : first + c1],
                    COPY,
                    scale=coef[:, col : col + 1],
                )

        grouped = {}

        def interleave(o, g, c0, c1, on_scalar=False):
            grouped[o, g, c0] = sb.tile(
                [P, PACK * (c1 - c0)], BF16, name="grouped%d%d_%d" % (o, g, c0), tag="grouped%d%d_%d" % (o, g, c0), align_bytes=64
            )
            dst, src = interleave_views(grouped[o, g, c0][:], planes[o, g, c0][:, :, :])
            if on_scalar:
                nc.scalar.copy(dst, src)
            else:
                nc.vector.tensor_copy(dst, src)

        def quantize_group(o, g, c0, c1):
            quantize(g, place(o, c0), c1 - c0, grouped[o, g, c0][:])

        acc = {}

        def second_product(i, g):
            if g == 0:
                acc[i] = bank(i, "acc%d" % i)
            a_cols = slice(place(A, i * P), place(A, i * P) + P)
            vv_cols = slice(place(VV, 0), place(VV, 0) + N)
            nc.tensor.matmul_mx(
                acc[i][:],
                lhsT=codes[g][:, a_cols].bitcast(FP8X4),
                lhsT_scale=scale[g][:, a_cols],
                rhs=codes[g][:, vv_cols].bitcast(FP8X4),
                rhs_scale=scale[g][:, vv_cols],
                start=(g == 0),
                stop=(g == PASSES - 1),
            )

        kept = {}

        def scale_old(i):
            kept[i] = sb.tile([P, N], F32, name="kept%d" % i, align_bytes=64)
            nc.scalar.activation(kept[i][:], old_sb[:, i, :], COPY, scale=KEEP)

        def finish_aside(i):
            gained = sb.tile([P, N], F32, name="gained%d" % i, align_bytes=64)
            nc.scalar.activation(gained[:], acc[i][:], COPY, scale=GAIN)
            result = sb.tile([P, N], F32, name="result%d" % i, tag="grouped%d%d_%d" % (A, 1, 3 * P), align_bytes=64)
            nc.gpsimd.tensor_tensor(result[:], gained[:], kept[i], ADD)
            nc.sync.dma_start(out[i * P : (i + 1) * P, :], result[:])

        def finish(i, c0=0, c1=N):
            result = sb.tile([P, c1 - c0], F32, name="result%d_%d" % (i, c0), align_bytes=64)
            nc.vector.scalar_tensor_tensor(result[:], acc[i][:, c0:c1], GAIN, kept[i][:, c0:c1], MULT, ADD)
            nc.sync.dma_start(out[i * P : (i + 1) * P, c0:c1], result[:])

        kept01 = sb.tile([P, 2 * N], F32, name="kept01", tag="w_grouped%d" % (3 * P), align_bytes=64)
        nc.gpsimd.tensor_scalar(kept01[:], old_sb[:, 0:2, :].rearrange("p i n -> p (i n)"), KEEP, 0.0, MULT, ADD)
        kept[0] = kept01[:, 0:N]
        kept[1] = kept01[:, N : 2 * N]
        for slots in ((0, 1), (2, 3)):
            for o in (VV, A):
                scale_planes(o, 1, 0, HALF, slots)
        g0 = (VV, 1, 0, HALF)
        g1 = (A, 1, 0, HALF)
        g2 = (VV, 0, HALF, N)
        g3 = (VV, 1, HALF, N)
        g4 = (A, 0, HALF, N)
        g5 = (A, 1, 2 * P, 3 * P)
        g6 = (A, 1, 3 * P, 4 * P)
        interleave(*g0)
        interleave(*g1)
        quantize_group(*g0)
        scale_planes(*g2, range(PACK))
        interleave(*g2)
        quantize_group(*g1)
        scale_planes(*g3, range(PACK))
        interleave(*g3)
        quantize_group(*g2)
        scale_planes(*g4, range(PACK))
        interleave(*g4)
        quantize_group(*g3)
        second_product(0, 0)
        second_product(0, 1)
        second_product(1, 0)
        second_product(1, 1)
        scale_planes(*g5, range(PACK))
        interleave(*g5)
        quantize_group(*g4)
        second_product(2, 0)
        second_product(3, 0)
        scale_planes(*g6, range(PACK))
        interleave(*g6)
        quantize_group(*g5)
        second_product(2, 1)
        quantize_group(*g6)
        second_product(3, 1)
        finish_aside(1)
        finish(0)
        scale_old(2)
        finish(2)
        scale_old(3)
        finish(3, 0, HALF)
        finish(3, HALF, N)
